import numpy as np
import ml_dtypes


def mxq(x, axis, fmt="e4m3"):
    dtype, down = {"e4m3": (ml_dtypes.float8_e4m3fn, 7), "e5m2": (ml_dtypes.float8_e5m2, 14)}[fmt]
    v = np.moveaxis(np.asarray(x, np.float32).astype(ml_dtypes.bfloat16).astype(np.float64), axis, -1)
    blocks = v.reshape(v.shape[:-1] + (-1, 32))
    amax = np.abs(blocks).max(-1, keepdims=True)
    byte = np.maximum(np.where(amax > 0, np.frexp(amax)[1] - 1 + 127, 0) - down, 1)
    scale = np.exp2(byte - 127.0)
    codes = (blocks / scale).astype(np.float32).astype(dtype).astype(np.float64)
    return np.moveaxis((codes * scale).reshape(v.shape), -1, axis)


WIDE = False


def mx_kscale(k):
    if not WIDE:
        return np.ones(k)
    levels = np.array([10, -10, 5, -5, 0])
    if k % 512:
        return np.exp2(np.random.permutation(np.resize(levels, k // 32))).repeat(32)
    a = np.empty((k // 512, 16))
    for p in range(k // 512):
        a[p, :8] = np.random.permutation(np.resize(levels, 8))
        for g in range(8):
            far = levels[np.abs(levels - a[p, g]) >= 10]
            a[p, g + 8] = far[np.random.randint(len(far))]
    return np.exp2(a.ravel()).repeat(32)


def f64(x):
    return np.asarray(x).astype(np.float64)


def striped(idx):
    return np.tile(np.asarray(idx).reshape(-1, 16).T, (8, 1)).astype(np.uint16)


def unstriped(offs):
    return offs[:16].T.reshape(-1).astype(np.int64)


E2M1 = np.array([0.0, 0.5, 1.0, 1.5, 2.0, 3.0, 4.0, 6.0, -0.0, -0.5, -1.0, -1.5, -2.0, -3.0, -4.0, -6.0])


def pack_weight(w, fmt):
    k, n = w.shape
    w = f64(np.asarray(w, np.float32).astype(ml_dtypes.bfloat16)).reshape(k // 32, 32, n)
    amax = np.abs(w).max(1)
    if fmt == "e4m3":
        byte = np.frexp(amax)[1] - 1 + 127 - 7
    else:
        mant, ex = np.frexp(amax / 6.0)
        byte = np.where(mant > 0.5, ex, ex - 1) + 127
    byte = np.clip(np.where(amax > 0, byte, 1), 1, 254)
    scaled = (w * np.exp2(127.0 - byte)[:, None, :]).reshape(k, n).astype(np.float32)
    by_word = np.ascontiguousarray(scaled.reshape(k // 512, 128, 4, n).transpose(0, 1, 3, 2))
    if fmt == "e4m3":
        words = by_word.astype(ml_dtypes.float8_e4m3fn).view(np.uint8)
    else:
        c = by_word.astype(ml_dtypes.float4_e2m1fn).view(np.uint8) & 0xF
        words = (c[..., 0::2] | (c[..., 1::2] << 4)).reshape(k // 512, 128, 2 * n)
    return np.ascontiguousarray(words), np.ascontiguousarray(byte.astype(np.uint8).reshape(k // 512, 16, n))


def unpack_weight(words, scales, fmt):
    g, _, n = scales.shape
    words = np.ascontiguousarray(words).reshape(g, 128, n, -1)
    if fmt == "e4m3":
        vals = words.view(ml_dtypes.float8_e4m3fn).astype(np.float64)
    else:
        nib = np.empty((g, 128, n, 4), np.uint8)
        nib[..., 0::2] = words & 0xF
        nib[..., 1::2] = words >> 4
        vals = E2M1[nib]
    vals = vals * np.repeat(np.exp2(scales.astype(np.float64) - 127.0), 8, axis=1)[..., None]
    return vals.transpose(0, 1, 3, 2).reshape(g * 512, n)


D, E, T, I, G, U, Q = 512, 512, 2048, 512, 64, 512, 128


def setup_inputs():
    n = np.random.standard_normal
    idx = np.random.permutation(T)[:I]
    idx2 = np.random.permutation(U)[:G]
    fd = mx_kscale(D)
    fe = mx_kscale(E)
    pgsump = pack_weight(n((D, U)) / fd[:, None], "e4m3")
    keysp = pack_weight(n((D, T)) / fd[:, None], "e4m3")
    valsp = pack_weight(n((E, T)) / fe[:, None], "e4m3")
    return {
        "pquery": (n((D, Q)) * 1.0 / np.sqrt(D) * fd[:, None]).astype(np.float32),
        "pgsum_words": pgsump[0],
        "pgsum_scales": pgsump[1],
        "query": (n((D, Q)) * 0.7 / np.sqrt(D) * fd[:, None]).astype(np.float32),
        "keys_words": keysp[0],
        "keys_scales": keysp[1],
        "even": (np.random.uniform(0.1, 0.6, (Q, 1))).astype(np.float32),
        "gout": (n((E, Q)) * 1 / np.sqrt(E) * fe[:, None]).astype(np.float32),
        "vals_words": valsp[0],
        "vals_scales": valsp[1],
        "dpquery": (n((D, Q)) * 1.0 / np.sqrt(D) * fd[:, None]).astype(np.float32),
        "base": (0.5 * n((Q, G))).astype(np.float32),
        "offs": striped(idx),
        "offs2": striped(idx2),
    }


def reference(pquery, pgsum_words, pgsum_scales, query, keys_words, keys_scales, even, gout, vals_words, vals_scales, dpquery, base, offs, offs2):
    idx = unstriped(offs)
    idx2 = unstriped(offs2)
    pgsumu = unpack_weight(pgsum_words, pgsum_scales, "e4m3")
    keysu = unpack_weight(keys_words, keys_scales, "e4m3")
    valsu = unpack_weight(vals_words, vals_scales, "e4m3")
    pqueryq = mxq(f64(pquery), 0, "e4m3")
    pgsumidx2g = pgsumu[:, idx2]
    b = pqueryq.T @ pgsumidx2g
    dpqueryq = mxq(f64(dpquery), 0, "e4m3")
    tb = dpqueryq.T @ pgsumidx2g
    pb = np.exp(b - np.max(b, axis=1, keepdims=True))
    zb = np.sum(pb, axis=1, keepdims=True)
    queryq = mxq(f64(query), 0, "e4m3")
    keysidxg = keysu[:, idx]
    a = queryq.T @ keysidxg
    pa = np.exp(a)
    s = pa.reshape(Q, G, I // G).sum(axis=2)
    goutq = mxq(f64(gout), 0, "e4m3")
    valsidxg = valsu[:, idx]
    c0 = goutq.T @ valsidxg
    m1 = (pa * c0).reshape(Q, G, I // G).sum(axis=2) / s
    dzb = np.sum(m1 * (1.0 - f64(even)) * pb / np.square(zb) * (-1.0), axis=1, keepdims=True)
    dpb = m1 * (1.0 - f64(even)) / zb + dzb
    xpb = tb * pb
    xzb = np.sum(xpb, axis=1, keepdims=True)
    xdzb = np.sum((xpb * m1 * (1.0 - f64(even)) - xzb * zb * 2.0 * m1 * (1.0 - f64(even)) * pb / np.square(zb)) / np.square(zb) * (-1.0), axis=1, keepdims=True)
    xdpb = xzb * m1 * (1.0 - f64(even)) / np.square(zb) * (-1.0) + xdzb
    xdb = xdpb * pb + xpb * dpb
    y = xdb * 256.0 + f64(base)
    return y

@@ -1,0 +1,181 @@
+from contextlib import ExitStack
+
+import concourse.mybir as mybir
+
+D, T, I, G, U, Q = 512, 2048, 512, 64, 512, 128
+FLOPS = 2 * D * Q * (2 * I + 2 * G)
+
+F32 = mybir.dt.float32
+BF16 = mybir.dt.bfloat16
+I32 = mybir.dt.int32
+U32 = mybir.dt.uint32
+U16 = mybir.dt.uint16
+U8 = mybir.dt.uint8
+FP8X4 = mybir.dt.float8_e4m3fn_x4
+ALU = mybir.AluOpType
+ACT = mybir.ActivationFunctionType
+AX = mybir.AxisListType
+
+P = 128
+PACK = 4
+SLOTS = I // G
+HALF = I // 2
+
+
+def tile_attend_hvevenmass_b_kernel(tc, pquery, pgsum_words, pgsum_scales, query, keys_words, keys_scales, even,
+                                     gout, vals_words, vals_scales, dpquery, base, offs, offs2, out):
+    nc = tc.nc
+    with ExitStack() as ctx:
+        sb = ctx.enter_context(tc.tile_pool(name="sb", bufs=1))
+        reuse = ctx.enter_context(tc.tile_pool(name="reuse", bufs=1))
+        ps = ctx.enter_context(tc.psum_pool(name="ps", bufs=1))
+
+        def tile(name, shape, dtype):
+            return sb.tile(shape, dtype, name=name, align_bytes=64)
+
+        def load_words(name, words, width):
+            t = tile(name, [P, width], U32)
+            nc.sync.dma_start(out=t[:].bitcast(I32), in_=words[0].rearrange("p n t -> p (n t)").bitcast(I32))
+            return t
+
+        def zero(t):
+            nc.vector.memset(t[:].bitcast(I32), 0)
+
+        def load_scales(queue, t, scales):
+            for quad in range(4):
+                queue.dma_start(out=t[32 * quad : 32 * quad + 4, :].bitcast(I32),
+                                in_=scales[0, 4 * quad : 4 * quad + 4, :].bitcast(I32))
+
+        def load_columns(name, x):
+            t = tile(name, [P, PACK, Q], F32)
+            nc.sync.dma_start(out=t[:], in_=x.rearrange("(p j) q -> p j q", j=PACK))
+            return t
+
+        def interleave(dst, raw):
+            nc.scalar.copy(out=dst, in_=raw[:].rearrange("p j q -> p q j"))
+
+        def quantized(name, raw, scales):
+            grouped = tile(name + "_bf", [P, Q, PACK], BF16)
+            interleave(grouped[:], raw)
+            codes = tile(name + "_codes", [P, Q], U32)
+            nc.vector.quantize_mx(out=codes[:].bitcast(FP8X4), scales=scales[:],
+                                  in_=grouped[:].rearrange("p q j -> p (q j)"))
+            return codes, scales
+
+        def product(acc, lhs, rhs_words, rhs_scales):
+            nc.tensor.matmul_mx(out=acc, lhsT=lhs[0][:].bitcast(FP8X4), lhsT_scale=lhs[1][:],
+                                rhs=rhs_words.bitcast(FP8X4), rhs_scale=rhs_scales, start=True, stop=True)
+
+        ks = tile("ks", [P, T], U8)
+        zero(ks)
+        warm = tile("warm", [P, 1], F32)
+        nc.vector.memset(warm[:], 0.0)
+        vs = tile("vs", [P, T], U8)
+        zero(vs)
+        gs = reuse.tile([P, U], U8, name="gs", offset=0, align_bytes=64)
+        zero(gs)
+        warm_out = tile("warm_out", [P, 1], F32)
+        nc.scalar.activation(out=warm_out[:], in_=warm[:], func=ACT.Exp)
+
+        even_t = tile("even_t", [P, 1], F32)
+        nc.gpsimd.dma_start(out=even_t[:], in_=even)
+        base_t = tile("base_t", [P, G], F32)
+        nc.gpsimd.dma_start(out=base_t[:], in_=base)
+        gain = tile("gain", [P, 1], F32)
+        nc.gpsimd.tensor_scalar(out=gain[:], in0=even_t[:], scalar1=-256.0, scalar2=256.0, op0=ALU.mult, op1=ALU.add)
+
+        offs_t = sb.tile([P, I // 16], U16, name="offs_t")
+        nc.sync.dma_start(offs_t[:], offs)
+        offs2_t = sb.tile([P, G // 16], U16, name="offs2_t")
+        nc.sync.dma_start(offs2_t[:], offs2)
+        load_scales(nc.sync, ks, keys_scales)
+        kw = load_words("kw", keys_words, T)
+        q_raw = load_columns("q_raw", query)
+        pq_raw = load_columns("pq_raw", pquery)
+        load_scales(nc.sync, vs, vals_scales)
+        gw = load_words("gw", pgsum_words, U)
+        dp_raw = load_columns("dp_raw", dpquery)
+        go_raw = load_columns("go_raw", gout)
+        load_scales(nc.sync, gs, pgsum_scales)
+        vw = load_words("vw", vals_words, T)
+
+        ksg = tile("ksg", [P, I], U8)
+        nc.vector.tensor_copy(out=ksg[:], in_=ks[:].indirect(offs_t[:]))
+        kwg = tile("kwg", [P, I], U32)
+        nc.vector.tensor_copy(out=kwg[:], in_=kw[:].indirect(offs_t[:]))
+        q_mx = quantized("q", q_raw, tile("q_scales", [P, Q], U8))
+        a_ps = ps.tile([P, I], F32, name="a_ps")
+        product(a_ps[:], q_mx, kwg[:], ksg[:])
+        vsg = tile("vsg", [P, I], U8)
+        nc.vector.tensor_copy(out=vsg[:], in_=vs[:].indirect(offs_t[:]))
+        pq_mx = quantized("pq", pq_raw, sb.tile([P, Q], U8, name="pq_scales", tag="vs", align_bytes=64))
+        pa = tile("pa", [P, I], F32)
+        nc.scalar.activation(out=pa[:], in_=a_ps[:], func=ACT.Exp)
+
+        gwg = tile("gwg", [P, G], U32)
+        nc.vector.tensor_copy(out=gwg[:], in_=gw[:].indirect(offs2_t[:]))
+        gsg = tile("gsg", [P, G], U8)
+        nc.vector.tensor_copy(out=gsg[:], in_=gs[:].indirect(offs2_t[:]))
+        b_ps = ps.tile([P, G], F32, name="b_ps")
+        product(b_ps[:], pq_mx, gwg[:], gsg[:])
+        s = reuse.tile([P, G], F32, name="s", offset=0, align_bytes=64)
+        nc.vector.tensor_reduce(out=s[:], in_=pa[:].rearrange("p (g j) -> p g j", j=SLOTS), axis=AX.X, op=ALU.add)
+        nmax = tile("nmax", [P, 1], F32)
+        nc.vector.tensor_reduce(out=nmax[:], in_=b_ps[:], axis=AX.X, op=ALU.max, negate=True)
+        dp_mx = quantized("dp", dp_raw, reuse.tile([P, Q], U8, name="dp_scales", offset=256, align_bytes=64))
+        tb_ps = ps.tile([P, G], F32, name="tb_ps")
+        product(tb_ps[:], dp_mx, gwg[:], gsg[:])
+        pb = tile("pb", [P, G], F32)
+        zb = tile("zb", [P, 1], F32)
+        nc.scalar.activation(out=pb[:], in_=b_ps[:], func=ACT.Exp, bias=nmax[:], accum_out=zb[:])
+        r = tile("r", [P, G], F32)
+        nc.vector.reciprocal(out=r[:], in_=s[:])
+        rz = tile("rz", [P, 1], F32)
+        nc.vector.reciprocal(out=rz[:], in_=zb[:])
+        go_mx = quantized("go", go_raw, reuse.tile([P, Q], U8, name="go_scales", offset=384, align_bytes=64))
+        pp = tile("pp", [P, 2, G], F32)
+        nc.vector.tensor_scalar(out=pp[:, 0, :], in0=pb[:], scalar1=rz[:], scalar2=None, op0=ALU.mult)
+        pg = tile("pg", [P, G], F32)
+        nc.vector.tensor_scalar(out=pg[:], in0=pb[:], scalar1=rz[:], scalar2=gain[:], op0=ALU.mult, op1=ALU.mult)
+
+        vwg = tile("vwg", [P, I], U32)
+        c_ps = [ps.tile([P, HALF], F32, name="c_ps%d" % h) for h in range(2)]
+        for h in range(2):
+            cols = slice(h * HALF, (h + 1) * HALF)
+            nc.vector.tensor_copy(out=vwg[:, cols], in_=vw[:].indirect(offs_t[:, h * HALF // 16 : (h + 1) * HALF // 16]))
+            product(c_ps[h][:], go_mx, vwg[:, cols], vsg[:, cols])
+        xp = sb.tile([P, G], F32, name="xp", tag="vw", align_bytes=64)
+        tmean = tile("tmean", [P, 1], F32)
+        nc.vector.scalar_tensor_tensor(out=xp[:], in0=tb_ps[:], scalar=1.0, in1=pp[:, 0, :], op0=ALU.mult, op1=ALU.mult,
+                                       accum_out=tmean[:])
+        nc.vector.scalar_tensor_tensor(out=pp[:, 1, :], in0=tb_ps[:], scalar=tmean[:], in1=pg[:],
+                                       op0=ALU.subtract, op1=ALU.mult)
+        rr = tile("rr", [P, 2, G], F32)
+        nc.vector.tensor_tensor(out=rr[:], in0=pp[:], in1=r[:].unsqueeze(1).to_broadcast([P, 2, G]), op=ALU.mult)
+        pac = tile("pac", [P, I], F32)
+        for h in range(2):
+            cols = slice(h * HALF, (h + 1) * HALF)
+            nc.vector.tensor_tensor(out=pac[:, cols], in0=c_ps[h][:], in1=pa[:, cols], op=ALU.mult)
+        n = tile("n", [P, G], F32)
+        for h in range(2):
+            nc.vector.tensor_reduce(out=n[:, h * G // 2 : (h + 1) * G // 2],
+                                    in_=pac[:, h * HALF : (h + 1) * HALF].rearrange("p (g j) -> p g j", j=SLOTS),
+                                    axis=AX.X, op=ALU.add)
+
+        mp = tile("mp", [P, G], F32)
+        s1 = tile("s1", [P, 1], F32)
+        nc.vector.scalar_tensor_tensor(out=mp[:], in0=n[:], scalar=1.0, in1=rr[:, 0, :], op0=ALU.mult, op1=ALU.mult,
+                                       accum_out=s1[:])
+        t1 = tile("t1", [P, G], F32)
+        c2 = tile("c2", [P, 1], F32)
+        nc.vector.scalar_tensor_tensor(out=t1[:], in0=n[:], scalar=1.0, in1=rr[:, 1, :], op0=ALU.mult, op1=ALU.mult,
+                                       accum_out=c2[:])
+        t2 = tile("t2", [P, G], F32)
+        nc.vector.scalar_tensor_tensor(out=t2[:], in0=pp[:, 1, :], scalar=s1[:], in1=base_t[:], op0=ALU.mult,
+                                       op1=ALU.subtract)
+        t3 = tile("t3", [P, G], F32)
+        nc.vector.scalar_tensor_tensor(out=t3[:], in0=pp[:, 0, :], scalar=c2[:], in1=t1[:], op0=ALU.mult,
+                                       op1=ALU.subtract)
+        y = tile("y", [P, G], F32)
+        nc.vector.scalar_tensor_tensor(out=y[:], in0=t2[:], scalar=-1.0, in1=t3[:], op0=ALU.mult, op1=ALU.subtract)
+        nc.sync.dma_start(out=out, in_=y[:])

@@ -20,6 +20,7 @@ P = 128
 PACK = 4
 SLOTS = I // G
 HALF = I // 2
+KEYS_ROW, VALS_ROW = 4, 8
 
 
 def tile_attend_hvevenmass_b_kernel(tc, pquery, pgsum_words, pgsum_scales, query, keys_words, keys_scales, even,
@@ -33,29 +34,28 @@ def tile_attend_hvevenmass_b_kernel(tc, pquery, pgsum_words, pgsum_scales, query
         def tile(name, shape, dtype):
             return sb.tile(shape, dtype, name=name, align_bytes=64)
 
-        def load_words(name, words, width):
-            t = tile(name, [P, width], U32)
+        def load_words(t, words):
             nc.sync.dma_start(out=t[:].bitcast(I32), in_=words[0].rearrange("p n t -> p (n t)").bitcast(I32))
             return t
 
         def zero(t):
             nc.vector.memset(t[:].bitcast(I32), 0)
 
-        def load_scales(queue, t, scales):
-            for quad in range(4):
-                queue.dma_start(out=t[32 * quad : 32 * quad + 4, :].bitcast(I32),
-                                in_=scales[0, 4 * quad : 4 * quad + 4, :].bitcast(I32))
+        def load_scales(queue, t, scales, first):
+            for row in range(4):
+                queue.dma_start(out=t[first + row : P : 32, :].bitcast(I32),
+                                in_=scales[0, row : 16 : 4, :].bitcast(I32))
 
-        def load_columns(name, x):
-            t = tile(name, [P, PACK, Q], F32)
+        def load_columns(name, x, tag):
+            t = sb.tile([P, PACK, Q], F32, name=name, tag=tag, align_bytes=64)
             nc.sync.dma_start(out=t[:], in_=x.rearrange("(p j) q -> p j q", j=PACK))
             return t
 
         def interleave(dst, raw):
             nc.scalar.copy(out=dst, in_=raw[:].rearrange("p j q -> p q j"))
 
-        def quantized(name, raw, scales):
-            grouped = tile(name + "_bf", [P, Q, PACK], BF16)
+        def quantized(name, raw, grouped):
+            scales = tile(name + "_scales", [P, Q], U8)
             interleave(grouped[:], raw)
             codes = tile(name + "_codes", [P, Q], U32)
             nc.vector.quantize_mx(out=codes[:].bitcast(FP8X4), scales=scales[:],
@@ -66,19 +66,23 @@ def tile_attend_hvevenmass_b_kernel(tc, pquery, pgsum_words, pgsum_scales, query
             nc.tensor.matmul_mx(out=acc, lhsT=lhs[0][:].bitcast(FP8X4), lhsT_scale=lhs[1][:],
                                 rhs=rhs_words.bitcast(FP8X4), rhs_scale=rhs_scales, start=True, stop=True)
 
+        def placed(name, shape, dtype, offset):
+            return reuse.tile(shape, dtype, name=name, offset=offset, align_bytes=64)
+
         ks = tile("ks", [P, T], U8)
         zero(ks)
+        gs = tile("gs", [P, U], U8)
+        zero(gs)
         warm = tile("warm", [P, 1], F32)
         nc.vector.memset(warm[:], 0.0)
-        vs = tile("vs", [P, T], U8)
+        vs = placed("vs", [P, T], U8, 0)
         zero(vs)
-        gs = reuse.tile([P, U], U8, name="gs", offset=0, align_bytes=64)
-        zero(gs)
         warm_out = tile("warm_out", [P, 1], F32)
         nc.scalar.activation(out=warm_out[:], in_=warm[:], func=ACT.Exp)
 
         even_t = tile("even_t", [P, 1], F32)
         nc.gpsimd.dma_start(out=even_t[:], in_=even)
+        load_scales(nc.gpsimd, gs, pgsum_scales, 0)
         base_t = tile("base_t", [P, G], F32)
         nc.gpsimd.dma_start(out=base_t[:], in_=base)
         gain = tile("gain", [P, 1], F32)
@@ -86,95 +90,94 @@ def tile_attend_hvevenmass_b_kernel(tc, pquery, pgsum_words, pgsum_scales, query
 
         offs_t = sb.tile([P, I // 16], U16, name="offs_t")
         nc.sync.dma_start(offs_t[:], offs)
+        q_raw = load_columns("q_raw", query, "q")
+        pq_raw = load_columns("pq_raw", pquery, "pq")
+        load_scales(nc.sync, ks, keys_scales, KEYS_ROW)
+        kw = load_words(tile("kw", [P, T], U32), keys_words)
+        gw = load_words(tile("gw", [P, U], U32), pgsum_words)
         offs2_t = sb.tile([P, G // 16], U16, name="offs2_t")
         nc.sync.dma_start(offs2_t[:], offs2)
-        load_scales(nc.sync, ks, keys_scales)
-        kw = load_words("kw", keys_words, T)
-        q_raw = load_columns("q_raw", query)
-        pq_raw = load_columns("pq_raw", pquery)
-        load_scales(nc.sync, vs, vals_scales)
-        gw = load_words("gw", pgsum_words, U)
-        dp_raw = load_columns("dp_raw", dpquery)
-        go_raw = load_columns("go_raw", gout)
-        load_scales(nc.sync, gs, pgsum_scales)
-        vw = load_words("vw", vals_words, T)
+        load_scales(nc.sync, vs, vals_scales, VALS_ROW)
+        vw = load_words(placed("vw", [P, T], U32, 2 * T), vals_words)
+        go_raw = load_columns("go_raw", gout, "go")
+        dp_raw = load_columns("dp_raw", dpquery, "dp")
 
+        q_mx = quantized("q", q_raw, tile("q_bf", [P, Q, PACK], BF16))
+        pq_mx = quantized("pq", pq_raw, tile("pq_bf", [P, Q, PACK], BF16))
         ksg = tile("ksg", [P, I], U8)
         nc.vector.tensor_copy(out=ksg[:], in_=ks[:].indirect(offs_t[:]))
         kwg = tile("kwg", [P, I], U32)
-        nc.vector.tensor_copy(out=kwg[:], in_=kw[:].indirect(offs_t[:]))
-        q_mx = quantized("q", q_raw, tile("q_scales", [P, Q], U8))
-        a_ps = ps.tile([P, I], F32, name="a_ps")
-        product(a_ps[:], q_mx, kwg[:], ksg[:])
-        vsg = tile("vsg", [P, I], U8)
-        nc.vector.tensor_copy(out=vsg[:], in_=vs[:].indirect(offs_t[:]))
-        pq_mx = quantized("pq", pq_raw, sb.tile([P, Q], U8, name="pq_scales", tag="vs", align_bytes=64))
         pa = tile("pa", [P, I], F32)
-        nc.scalar.activation(out=pa[:], in_=a_ps[:], func=ACT.Exp)
+        for h in range(2):
+            cols = slice(h * HALF, (h + 1) * HALF)
+            nc.vector.tensor_copy(out=kwg[:, cols],
+                                  in_=kw[:].indirect(offs_t[:, h * HALF // 16 : (h + 1) * HALF // 16]))
+            a_ps = ps.tile([P, HALF], F32, name="a_ps%d" % h)
+            product(a_ps[:], q_mx, kwg[:, cols], ksg[KEYS_ROW:, cols])
+            nc.scalar.activation(out=pa[:, cols], in_=a_ps[:], func=ACT.Exp)
 
         gwg = tile("gwg", [P, G], U32)
         nc.vector.tensor_copy(out=gwg[:], in_=gw[:].indirect(offs2_t[:]))
-        gsg = tile("gsg", [P, G], U8)
+        vsg = tile("vsg", [P, I], U8)
+        nc.vector.tensor_copy(out=vsg[:], in_=vs[:].indirect(offs_t[:]))
+        gsg = placed("gsg", [P, G], U8, 0)
         nc.vector.tensor_copy(out=gsg[:], in_=gs[:].indirect(offs2_t[:]))
         b_ps = ps.tile([P, G], F32, name="b_ps")
         product(b_ps[:], pq_mx, gwg[:], gsg[:])
-        s = reuse.tile([P, G], F32, name="s", offset=0, align_bytes=64)
+        s = placed("s", [P, G], F32, 64)
         nc.vector.tensor_reduce(out=s[:], in_=pa[:].rearrange("p (g j) -> p g j", j=SLOTS), axis=AX.X, op=ALU.add)
         nmax = tile("nmax", [P, 1], F32)
         nc.vector.tensor_reduce(out=nmax[:], in_=b_ps[:], axis=AX.X, op=ALU.max, negate=True)
-        dp_mx = quantized("dp", dp_raw, reuse.tile([P, Q], U8, name="dp_scales", offset=256, align_bytes=64))
-        tb_ps = ps.tile([P, G], F32, name="tb_ps")
-        product(tb_ps[:], dp_mx, gwg[:], gsg[:])
         pb = tile("pb", [P, G], F32)
         zb = tile("zb", [P, 1], F32)
         nc.scalar.activation(out=pb[:], in_=b_ps[:], func=ACT.Exp, bias=nmax[:], accum_out=zb[:])
-        r = tile("r", [P, G], F32)
-        nc.vector.reciprocal(out=r[:], in_=s[:])
-        rz = tile("rz", [P, 1], F32)
-        nc.vector.reciprocal(out=rz[:], in_=zb[:])
-        go_mx = quantized("go", go_raw, reuse.tile([P, Q], U8, name="go_scales", offset=384, align_bytes=64))
-        pp = tile("pp", [P, 2, G], F32)
-        nc.vector.tensor_scalar(out=pp[:, 0, :], in0=pb[:], scalar1=rz[:], scalar2=None, op0=ALU.mult)
-        pg = tile("pg", [P, G], F32)
-        nc.vector.tensor_scalar(out=pg[:], in0=pb[:], scalar1=rz[:], scalar2=gain[:], op0=ALU.mult, op1=ALU.mult)
 
         vwg = tile("vwg", [P, I], U32)
+        nc.vector.tensor_copy(out=vwg[:], in_=vw[:].indirect(offs_t[:]))
+        rz = placed("rz", [P, 1], F32, 2 * T)
+        nc.vector.reciprocal(out=rz[:], in_=zb[:])
+        go_mx = quantized("go", go_raw, placed("go_bf", [P, Q, PACK], BF16, T))
         c_ps = [ps.tile([P, HALF], F32, name="c_ps%d" % h) for h in range(2)]
         for h in range(2):
             cols = slice(h * HALF, (h + 1) * HALF)
-            nc.vector.tensor_copy(out=vwg[:, cols], in_=vw[:].indirect(offs_t[:, h * HALF // 16 : (h + 1) * HALF // 16]))
-            product(c_ps[h][:], go_mx, vwg[:, cols], vsg[:, cols])
-        xp = sb.tile([P, G], F32, name="xp", tag="vw", align_bytes=64)
-        tmean = tile("tmean", [P, 1], F32)
-        nc.vector.scalar_tensor_tensor(out=xp[:], in0=tb_ps[:], scalar=1.0, in1=pp[:, 0, :], op0=ALU.mult, op1=ALU.mult,
-                                       accum_out=tmean[:])
-        nc.vector.scalar_tensor_tensor(out=pp[:, 1, :], in0=tb_ps[:], scalar=tmean[:], in1=pg[:],
-                                       op0=ALU.subtract, op1=ALU.mult)
-        rr = tile("rr", [P, 2, G], F32)
-        nc.vector.tensor_tensor(out=rr[:], in0=pp[:], in1=r[:].unsqueeze(1).to_broadcast([P, 2, G]), op=ALU.mult)
+            product(c_ps[h][:], go_mx, vwg[:, cols], vsg[VALS_ROW:, cols])
+        dp_mx = quantized("dp", dp_raw, tile("dp_bf", [P, Q, PACK], BF16))
+        tb_ps = ps.tile([P, G], F32, name="tb_ps")
+        product(tb_ps[:], dp_mx, gwg[:], gsg[:])
+        share = sb.tile([P, 2, 2, G], F32, name="share", tag="dp", align_bytes=64)
+        r = placed("r", [P, G], F32, T)
+        nc.vector.reciprocal(out=r[:], in_=s[:])
+        nc.scalar.activation(out=share[:, 0, 0, :], in_=pb[:], func=ACT.Copy, scale=rz[:])
+        nc.scalar.activation(out=share[:, 0, 1, :], in_=share[:, 0, 0, :], func=ACT.Copy, scale=gain[:])
+        nc.vector.tensor_tensor(out=share[:, 1], in0=share[:, 0], in1=r[:].unsqueeze(1).to_broadcast([P, 2, G]),
+                                op=ALU.mult)
         pac = tile("pac", [P, I], F32)
         for h in range(2):
             cols = slice(h * HALF, (h + 1) * HALF)
             nc.vector.tensor_tensor(out=pac[:, cols], in0=c_ps[h][:], in1=pa[:, cols], op=ALU.mult)
+        xp = tile("xp", [P, G], F32)
+        tmean = tile("tmean", [P, 1], F32)
+        nc.vector.scalar_tensor_tensor(out=xp[:], in0=tb_ps[:], scalar=1.0, in1=share[:, 0, 0, :], op0=ALU.mult,
+                                       op1=ALU.mult, accum_out=tmean[:])
         n = tile("n", [P, G], F32)
-        for h in range(2):
-            nc.vector.tensor_reduce(out=n[:, h * G // 2 : (h + 1) * G // 2],
-                                    in_=pac[:, h * HALF : (h + 1) * HALF].rearrange("p (g j) -> p g j", j=SLOTS),
-                                    axis=AX.X, op=ALU.add)
+        nc.vector.tensor_reduce(out=n[:], in_=pac[:].rearrange("p (g j) -> p g j", j=SLOTS), axis=AX.X, op=ALU.add)
+        moved = tile("moved", [P, 2, G], F32)
+        nc.vector.scalar_tensor_tensor(out=moved[:], in0=tb_ps[:].unsqueeze(1).to_broadcast([P, 2, G]), scalar=tmean[:],
+                                       in1=share[:, :, 1, :], op0=ALU.subtract, op1=ALU.mult)
 
         mp = tile("mp", [P, G], F32)
         s1 = tile("s1", [P, 1], F32)
-        nc.vector.scalar_tensor_tensor(out=mp[:], in0=n[:], scalar=1.0, in1=rr[:, 0, :], op0=ALU.mult, op1=ALU.mult,
+        nc.vector.scalar_tensor_tensor(out=mp[:], in0=n[:], scalar=1.0, in1=share[:, 1, 0, :], op0=ALU.mult, op1=ALU.mult,
                                        accum_out=s1[:])
         t1 = tile("t1", [P, G], F32)
         c2 = tile("c2", [P, 1], F32)
-        nc.vector.scalar_tensor_tensor(out=t1[:], in0=n[:], scalar=1.0, in1=rr[:, 1, :], op0=ALU.mult, op1=ALU.mult,
+        nc.vector.scalar_tensor_tensor(out=t1[:], in0=n[:], scalar=1.0, in1=moved[:, 1, :], op0=ALU.mult, op1=ALU.mult,
                                        accum_out=c2[:])
         t2 = tile("t2", [P, G], F32)
-        nc.vector.scalar_tensor_tensor(out=t2[:], in0=pp[:, 1, :], scalar=s1[:], in1=base_t[:], op0=ALU.mult,
+        nc.vector.scalar_tensor_tensor(out=t2[:], in0=moved[:, 0, :], scalar=s1[:], in1=base_t[:], op0=ALU.mult,
                                        op1=ALU.subtract)
         t3 = tile("t3", [P, G], F32)
-        nc.vector.scalar_tensor_tensor(out=t3[:], in0=pp[:, 0, :], scalar=c2[:], in1=t1[:], op0=ALU.mult,
+        nc.vector.scalar_tensor_tensor(out=t3[:], in0=share[:, 0, 0, :], scalar=c2[:], in1=t1[:], op0=ALU.mult,
                                        op1=ALU.subtract)
         y = tile("y", [P, G], F32)
         nc.vector.scalar_tensor_tensor(out=y[:], in0=t2[:], scalar=-1.0, in1=t3[:], op0=ALU.mult, op1=ALU.subtract)

@@ -82,7 +82,6 @@ def tile_attend_hvevenmass_b_kernel(tc, pquery, pgsum_words, pgsum_scales, query
 
         even_t = tile("even_t", [P, 1], F32)
         nc.gpsimd.dma_start(out=even_t[:], in_=even)
-        load_scales(nc.gpsimd, gs, pgsum_scales, 0)
         base_t = tile("base_t", [P, G], F32)
         nc.gpsimd.dma_start(out=base_t[:], in_=base)
         gain = tile("gain", [P, 1], F32)
@@ -98,7 +97,8 @@ def tile_attend_hvevenmass_b_kernel(tc, pquery, pgsum_words, pgsum_scales, query
         offs2_t = sb.tile([P, G // 16], U16, name="offs2_t")
         nc.sync.dma_start(offs2_t[:], offs2)
         load_scales(nc.sync, vs, vals_scales, VALS_ROW)
-        vw = load_words(placed("vw", [P, T], U32, 2 * T), vals_words)
+        vw = load_words(tile("vw", [P, T], U32), vals_words)
+        load_scales(nc.sync, gs, pgsum_scales, 0)
         go_raw = load_columns("go_raw", gout, "go")
         dp_raw = load_columns("dp_raw", dpquery, "dp")
 
@@ -120,54 +120,54 @@ def tile_attend_hvevenmass_b_kernel(tc, pquery, pgsum_words, pgsum_scales, query
         nc.vector.tensor_copy(out=gwg[:], in_=gw[:].indirect(offs2_t[:]))
         vsg = tile("vsg", [P, I], U8)
         nc.vector.tensor_copy(out=vsg[:], in_=vs[:].indirect(offs_t[:]))
-        gsg = placed("gsg", [P, G], U8, 0)
-        nc.vector.tensor_copy(out=gsg[:], in_=gs[:].indirect(offs2_t[:]))
-        b_ps = ps.tile([P, G], F32, name="b_ps")
-        product(b_ps[:], pq_mx, gwg[:], gsg[:])
         s = placed("s", [P, G], F32, 64)
         nc.vector.tensor_reduce(out=s[:], in_=pa[:].rearrange("p (g j) -> p g j", j=SLOTS), axis=AX.X, op=ALU.add)
-        nmax = tile("nmax", [P, 1], F32)
-        nc.vector.tensor_reduce(out=nmax[:], in_=b_ps[:], axis=AX.X, op=ALU.max, negate=True)
-        pb = tile("pb", [P, G], F32)
-        zb = tile("zb", [P, 1], F32)
-        nc.scalar.activation(out=pb[:], in_=b_ps[:], func=ACT.Exp, bias=nmax[:], accum_out=zb[:])
 
         vwg = tile("vwg", [P, I], U32)
         nc.vector.tensor_copy(out=vwg[:], in_=vw[:].indirect(offs_t[:]))
-        rz = placed("rz", [P, 1], F32, 2 * T)
-        nc.vector.reciprocal(out=rz[:], in_=zb[:])
+        gsg = tile("gsg", [P, G], U8)
+        nc.vector.tensor_copy(out=gsg[:], in_=gs[:].indirect(offs2_t[:]))
+        b_ps = ps.tile([P, G], F32, name="b_ps")
+        product(b_ps[:], pq_mx, gwg[:], gsg[:])
         go_mx = quantized("go", go_raw, placed("go_bf", [P, Q, PACK], BF16, T))
         c_ps = [ps.tile([P, HALF], F32, name="c_ps%d" % h) for h in range(2)]
         for h in range(2):
             cols = slice(h * HALF, (h + 1) * HALF)
             product(c_ps[h][:], go_mx, vwg[:, cols], vsg[VALS_ROW:, cols])
+        r = placed("r", [P, G], F32, T)
+        nc.vector.reciprocal(out=r[:], in_=s[:])
+        nmax = placed("nmax", [P, 1], F32, T + 256)
+        nc.vector.tensor_reduce(out=nmax[:], in_=b_ps[:], axis=AX.X, op=ALU.max, negate=True)
         dp_mx = quantized("dp", dp_raw, tile("dp_bf", [P, Q, PACK], BF16))
         tb_ps = ps.tile([P, G], F32, name="tb_ps")
         product(tb_ps[:], dp_mx, gwg[:], gsg[:])
-        share = sb.tile([P, 2, 2, G], F32, name="share", tag="dp", align_bytes=64)
-        r = placed("r", [P, G], F32, T)
-        nc.vector.reciprocal(out=r[:], in_=s[:])
-        nc.scalar.activation(out=share[:, 0, 0, :], in_=pb[:], func=ACT.Copy, scale=rz[:])
-        nc.scalar.activation(out=share[:, 0, 1, :], in_=share[:, 0, 0, :], func=ACT.Copy, scale=gain[:])
-        nc.vector.tensor_tensor(out=share[:, 1], in0=share[:, 0], in1=r[:].unsqueeze(1).to_broadcast([P, 2, G]),
-                                op=ALU.mult)
+        pbr = tile("pbr", [P, 2, G], F32)
+        zb = tile("zb", [P, 1], F32)
+        nc.scalar.activation(out=pbr[:, 0, :], in_=b_ps[:], func=ACT.Exp, bias=nmax[:], accum_out=zb[:])
+        rz = tile("rz", [P, 1], F32)
+        nc.vector.reciprocal(out=rz[:], in_=zb[:])
+        share = tile("share", [P, G], F32)
+        nc.scalar.activation(out=share[:], in_=pbr[:, 0, :], func=ACT.Copy, scale=rz[:])
+        nc.vector.tensor_tensor(out=pbr[:, 1, :], in0=pbr[:, 0, :], in1=r[:], op=ALU.mult)
         pac = tile("pac", [P, I], F32)
         for h in range(2):
             cols = slice(h * HALF, (h + 1) * HALF)
             nc.vector.tensor_tensor(out=pac[:, cols], in0=c_ps[h][:], in1=pa[:, cols], op=ALU.mult)
+        scaled = tile("scaled", [P, 2, G], F32)
+        nc.vector.tensor_scalar(out=scaled[:], in0=pbr[:], scalar1=rz[:], scalar2=gain[:], op0=ALU.mult, op1=ALU.mult)
         xp = tile("xp", [P, G], F32)
         tmean = tile("tmean", [P, 1], F32)
-        nc.vector.scalar_tensor_tensor(out=xp[:], in0=tb_ps[:], scalar=1.0, in1=share[:, 0, 0, :], op0=ALU.mult,
+        nc.vector.scalar_tensor_tensor(out=xp[:], in0=tb_ps[:], scalar=rz[:], in1=pbr[:, 0, :], op0=ALU.mult,
                                        op1=ALU.mult, accum_out=tmean[:])
         n = tile("n", [P, G], F32)
         nc.vector.tensor_reduce(out=n[:], in_=pac[:].rearrange("p (g j) -> p g j", j=SLOTS), axis=AX.X, op=ALU.add)
         moved = tile("moved", [P, 2, G], F32)
         nc.vector.scalar_tensor_tensor(out=moved[:], in0=tb_ps[:].unsqueeze(1).to_broadcast([P, 2, G]), scalar=tmean[:],
-                                       in1=share[:, :, 1, :], op0=ALU.subtract, op1=ALU.mult)
+                                       in1=scaled[:], op0=ALU.subtract, op1=ALU.mult)
 
         mp = tile("mp", [P, G], F32)
         s1 = tile("s1", [P, 1], F32)
-        nc.vector.scalar_tensor_tensor(out=mp[:], in0=n[:], scalar=1.0, in1=share[:, 1, 0, :], op0=ALU.mult, op1=ALU.mult,
+        nc.vector.scalar_tensor_tensor(out=mp[:], in0=n[:], scalar=rz[:], in1=pbr[:, 1, :], op0=ALU.mult, op1=ALU.mult,
                                        accum_out=s1[:])
         t1 = tile("t1", [P, G], F32)
         c2 = tile("c2", [P, 1], F32)
@@ -177,7 +177,7 @@ def tile_attend_hvevenmass_b_kernel(tc, pquery, pgsum_words, pgsum_scales, query
         nc.vector.scalar_tensor_tensor(out=t2[:], in0=moved[:, 0, :], scalar=s1[:], in1=base_t[:], op0=ALU.mult,
                                        op1=ALU.subtract)
         t3 = tile("t3", [P, G], F32)
-        nc.vector.scalar_tensor_tensor(out=t3[:], in0=share[:, 0, 0, :], scalar=c2[:], in1=t1[:], op0=ALU.mult,
+        nc.vector.scalar_tensor_tensor(out=t3[:], in0=share[:], scalar=c2[:], in1=t1[:], op0=ALU.mult,
                                        op1=ALU.subtract)
         y = tile("y", [P, G], F32)
         nc.vector.scalar_tensor_tensor(out=y[:], in0=t2[:], scalar=-1.0, in1=t3[:], op0=ALU.mult, op1=ALU.subtract)

from contextlib import ExitStack

import concourse.mybir as mybir

D, T, I, G, U, Q = 512, 2048, 512, 64, 512, 128
FLOPS = 2 * D * Q * (2 * I + 2 * G)

F32 = mybir.dt.float32
BF16 = mybir.dt.bfloat16
I32 = mybir.dt.int32
U32 = mybir.dt.uint32
U16 = mybir.dt.uint16
U8 = mybir.dt.uint8
FP8X4 = mybir.dt.float8_e4m3fn_x4
ALU = mybir.AluOpType
ACT = mybir.ActivationFunctionType
AX = mybir.AxisListType

P = 128
PACK = 4
SLOTS = I // G
HALF = I // 2
KEYS_ROW, VALS_ROW = 4, 8


def tile_attend_hvevenmass_b_kernel(tc, pquery, pgsum_words, pgsum_scales, query, keys_words, keys_scales, even,
                                     gout, vals_words, vals_scales, dpquery, base, offs, offs2, out):
    nc = tc.nc
    with ExitStack() as ctx:
        sb = ctx.enter_context(tc.tile_pool(name="sb", bufs=1))
        reuse = ctx.enter_context(tc.tile_pool(name="reuse", bufs=1))
        ps = ctx.enter_context(tc.psum_pool(name="ps", bufs=1))

        def tile(name, shape, dtype):
            return sb.tile(shape, dtype, name=name, align_bytes=64)

        def load_words(t, words):
            nc.sync.dma_start(out=t[:].bitcast(I32), in_=words[0].rearrange("p n t -> p (n t)").bitcast(I32))
            return t

        def zero(t):
            nc.vector.memset(t[:].bitcast(I32), 0)

        def load_scales(queue, t, scales, first):
            for row in range(4):
                queue.dma_start(out=t[first + row : P : 32, :].bitcast(I32),
                                in_=scales[0, row : 16 : 4, :].bitcast(I32))

        def load_columns(name, x, tag):
            t = sb.tile([P, PACK, Q], F32, name=name, tag=tag, align_bytes=64)
            nc.sync.dma_start(out=t[:], in_=x.rearrange("(p j) q -> p j q", j=PACK))
            return t

        def interleave(dst, raw):
            nc.scalar.copy(out=dst, in_=raw[:].rearrange("p j q -> p q j"))

        def quantized(name, raw, grouped):
            scales = tile(name + "_scales", [P, Q], U8)
            interleave(grouped[:], raw)
            codes = tile(name + "_codes", [P, Q], U32)
            nc.vector.quantize_mx(out=codes[:].bitcast(FP8X4), scales=scales[:],
                                  in_=grouped[:].rearrange("p q j -> p (q j)"))
            return codes, scales

        def product(acc, lhs, rhs_words, rhs_scales):
            nc.tensor.matmul_mx(out=acc, lhsT=lhs[0][:].bitcast(FP8X4), lhsT_scale=lhs[1][:],
                                rhs=rhs_words.bitcast(FP8X4), rhs_scale=rhs_scales, start=True, stop=True)

        def placed(name, shape, dtype, offset):
            return reuse.tile(shape, dtype, name=name, offset=offset, align_bytes=64)

        ks = tile("ks", [P, T], U8)
        zero(ks)
        gs = tile("gs", [P, U], U8)
        zero(gs)
        warm = tile("warm", [P, 1], F32)
        nc.vector.memset(warm[:], 0.0)
        vs = placed("vs", [P, T], U8, 0)
        zero(vs)
        warm_out = tile("warm_out", [P, 1], F32)
        nc.scalar.activation(out=warm_out[:], in_=warm[:], func=ACT.Exp)

        even_t = tile("even_t", [P, 1], F32)
        nc.gpsimd.dma_start(out=even_t[:], in_=even)
        base_t = tile("base_t", [P, G], F32)
        nc.gpsimd.dma_start(out=base_t[:], in_=base)
        gain = tile("gain", [P, 1], F32)
        nc.gpsimd.tensor_scalar(out=gain[:], in0=even_t[:], scalar1=-256.0, scalar2=256.0, op0=ALU.mult, op1=ALU.add)

        offs_t = sb.tile([P, I // 16], U16, name="offs_t")
        nc.sync.dma_start(offs_t[:], offs)
        q_raw = load_columns("q_raw", query, "q")
        pq_raw = load_columns("pq_raw", pquery, "pq")
        load_scales(nc.sync, ks, keys_scales, KEYS_ROW)
        kw = load_words(tile("kw", [P, T], U32), keys_words)
        gw = load_words(tile("gw", [P, U], U32), pgsum_words)
        offs2_t = sb.tile([P, G // 16], U16, name="offs2_t")
        nc.sync.dma_start(offs2_t[:], offs2)
        load_scales(nc.sync, vs, vals_scales, VALS_ROW)
        vw = load_words(tile("vw", [P, T], U32), vals_words)
        load_scales(nc.sync, gs, pgsum_scales, 0)
        go_raw = load_columns("go_raw", gout, "go")
        dp_raw = load_columns("dp_raw", dpquery, "dp")

        q_mx = quantized("q", q_raw, tile("q_bf", [P, Q, PACK], BF16))
        pq_mx = quantized("pq", pq_raw, tile("pq_bf", [P, Q, PACK], BF16))
        ksg = tile("ksg", [P, I], U8)
        nc.vector.tensor_copy(out=ksg[:], in_=ks[:].indirect(offs_t[:]))
        kwg = tile("kwg", [P, I], U32)
        pa = tile("pa", [P, I], F32)
        for h in range(2):
            cols = slice(h * HALF, (h + 1) * HALF)
            nc.vector.tensor_copy(out=kwg[:, cols],
                                  in_=kw[:].indirect(offs_t[:, h * HALF // 16 : (h + 1) * HALF // 16]))
            a_ps = ps.tile([P, HALF], F32, name="a_ps%d" % h)
            product(a_ps[:], q_mx, kwg[:, cols], ksg[KEYS_ROW:, cols])
            nc.scalar.activation(out=pa[:, cols], in_=a_ps[:], func=ACT.Exp)

        gwg = tile("gwg", [P, G], U32)
        nc.vector.tensor_copy(out=gwg[:], in_=gw[:].indirect(offs2_t[:]))
        vsg = tile("vsg", [P, I], U8)
        nc.vector.tensor_copy(out=vsg[:], in_=vs[:].indirect(offs_t[:]))
        s = placed("s", [P, G], F32, 64)
        nc.vector.tensor_reduce(out=s[:], in_=pa[:].rearrange("p (g j) -> p g j", j=SLOTS), axis=AX.X, op=ALU.add)

        vwg = tile("vwg", [P, I], U32)
        nc.vector.tensor_copy(out=vwg[:], in_=vw[:].indirect(offs_t[:]))
        gsg = tile("gsg", [P, G], U8)
        nc.vector.tensor_copy(out=gsg[:], in_=gs[:].indirect(offs2_t[:]))
        b_ps = ps.tile([P, G], F32, name="b_ps")
        product(b_ps[:], pq_mx, gwg[:], gsg[:])
        go_mx = quantized("go", go_raw, placed("go_bf", [P, Q, PACK], BF16, T))
        c_ps = [ps.tile([P, HALF], F32, name="c_ps%d" % h) for h in range(2)]
        for h in range(2):
            cols = slice(h * HALF, (h + 1) * HALF)
            product(c_ps[h][:], go_mx, vwg[:, cols], vsg[VALS_ROW:, cols])
        r = placed("r", [P, G], F32, T)
        nc.vector.reciprocal(out=r[:], in_=s[:])
        nmax = placed("nmax", [P, 1], F32, T + 256)
        nc.vector.tensor_reduce(out=nmax[:], in_=b_ps[:], axis=AX.X, op=ALU.max, negate=True)
        dp_mx = quantized("dp", dp_raw, tile("dp_bf", [P, Q, PACK], BF16))
        tb_ps = ps.tile([P, G], F32, name="tb_ps")
        product(tb_ps[:], dp_mx, gwg[:], gsg[:])
        pbr = tile("pbr", [P, 2, G], F32)
        zb = tile("zb", [P, 1], F32)
        nc.scalar.activation(out=pbr[:, 0, :], in_=b_ps[:], func=ACT.Exp, bias=nmax[:], accum_out=zb[:])
        rz = tile("rz", [P, 1], F32)
        nc.vector.reciprocal(out=rz[:], in_=zb[:])
        share = tile("share", [P, G], F32)
        nc.scalar.activation(out=share[:], in_=pbr[:, 0, :], func=ACT.Copy, scale=rz[:])
        nc.vector.tensor_tensor(out=pbr[:, 1, :], in0=pbr[:, 0, :], in1=r[:], op=ALU.mult)
        pac = tile("pac", [P, I], F32)
        for h in range(2):
            cols = slice(h * HALF, (h + 1) * HALF)
            nc.vector.tensor_tensor(out=pac[:, cols], in0=c_ps[h][:], in1=pa[:, cols], op=ALU.mult)
        scaled = tile("scaled", [P, 2, G], F32)
        nc.vector.tensor_scalar(out=scaled[:], in0=pbr[:], scalar1=rz[:], scalar2=gain[:], op0=ALU.mult, op1=ALU.mult)
        xp = tile("xp", [P, G], F32)
        tmean = tile("tmean", [P, 1], F32)
        nc.vector.scalar_tensor_tensor(out=xp[:], in0=tb_ps[:], scalar=rz[:], in1=pbr[:, 0, :], op0=ALU.mult,
                                       op1=ALU.mult, accum_out=tmean[:])
        n = tile("n", [P, G], F32)
        nc.vector.tensor_reduce(out=n[:], in_=pac[:].rearrange("p (g j) -> p g j", j=SLOTS), axis=AX.X, op=ALU.add)
        moved = tile("moved", [P, 2, G], F32)
        nc.vector.scalar_tensor_tensor(out=moved[:], in0=tb_ps[:].unsqueeze(1).to_broadcast([P, 2, G]), scalar=tmean[:],
                                       in1=scaled[:], op0=ALU.subtract, op1=ALU.mult)

        mp = tile("mp", [P, G], F32)
        s1 = tile("s1", [P, 1], F32)
        nc.vector.scalar_tensor_tensor(out=mp[:], in0=n[:], scalar=rz[:], in1=pbr[:, 1, :], op0=ALU.mult, op1=ALU.mult,
                                       accum_out=s1[:])
        t1 = tile("t1", [P, G], F32)
        c2 = tile("c2", [P, 1], F32)
        nc.vector.scalar_tensor_tensor(out=t1[:], in0=n[:], scalar=1.0, in1=moved[:, 1, :], op0=ALU.mult, op1=ALU.mult,
                                       accum_out=c2[:])
        t2 = tile("t2", [P, G], F32)
        nc.vector.scalar_tensor_tensor(out=t2[:], in0=moved[:, 0, :], scalar=s1[:], in1=base_t[:], op0=ALU.mult,
                                       op1=ALU.subtract)
        t3 = tile("t3", [P, G], F32)
        nc.vector.scalar_tensor_tensor(out=t3[:], in0=share[:], scalar=c2[:], in1=t1[:], op0=ALU.mult,
                                       op1=ALU.subtract)
        y = tile("y", [P, G], F32)
        nc.vector.scalar_tensor_tensor(out=y[:], in0=t2[:], scalar=-1.0, in1=t3[:], op0=ALU.mult, op1=ALU.subtract)
        nc.sync.dma_start(out=out, in_=y[:])
